import numpy as np
import ml_dtypes


def mxq(x, axis, fmt="e4m3"):
    dtype, down = {"e4m3": (ml_dtypes.float8_e4m3fn, 7), "e5m2": (ml_dtypes.float8_e5m2, 14)}[fmt]
    v = np.moveaxis(np.asarray(x, np.float32).astype(ml_dtypes.bfloat16).astype(np.float64), axis, -1)
    blocks = v.reshape(v.shape[:-1] + (-1, 32))
    amax = np.abs(blocks).max(-1, keepdims=True)
    byte = np.maximum(np.where(amax > 0, np.frexp(amax)[1] - 1 + 127, 0) - down, 1)
    scale = np.exp2(byte - 127.0)
    codes = (blocks / scale).astype(np.float32).astype(dtype).astype(np.float64)
    return np.moveaxis((codes * scale).reshape(v.shape), -1, axis)


WIDE = False


def mx_kscale(k):
    if not WIDE:
        return np.ones(k)
    levels = np.array([10, -10, 5, -5, 0])
    if k % 512:
        return np.exp2(np.random.permutation(np.resize(levels, k // 32))).repeat(32)
    a = np.empty((k // 512, 16))
    for p in range(k // 512):
        a[p, :8] = np.random.permutation(np.resize(levels, 8))
        for g in range(8):
            far = levels[np.abs(levels - a[p, g]) >= 10]
            a[p, g + 8] = far[np.random.randint(len(far))]
    return np.exp2(a.ravel()).repeat(32)


def f64(x):
    return np.asarray(x).astype(np.float64)


def striped(idx):
    return np.tile(idx.reshape(-1, 16).T, (8, 1)).astype(np.uint16)


def unstriped(offs):
    return offs[:16].T.reshape(-1).astype(np.int64)


def pack_weight(w):
    k, n = w.shape
    w = f64(np.asarray(w, np.float32).astype(ml_dtypes.bfloat16)).reshape(k // 32, 32, n)
    amax = np.abs(w).max(1)
    byte = np.clip(np.where(amax > 0, np.frexp(amax)[1] - 1 + 127 - 7, 1), 1, 254)
    scaled = (w * np.exp2(127.0 - byte)[:, None, :]).reshape(k, n).astype(np.float32)
    words = np.ascontiguousarray(scaled.reshape(k // 512, 128, 4, n).transpose(0, 1, 3, 2)).astype(ml_dtypes.float8_e4m3fn).view(np.uint8)
    return words, np.ascontiguousarray(byte.astype(np.uint8).reshape(k // 512, 16, n))


def unpack_weight(words, scales):
    g, p, n, _ = words.shape
    vals = np.ascontiguousarray(words).view(ml_dtypes.float8_e4m3fn).astype(np.float64) * np.repeat(np.exp2(scales.astype(np.float64) - 127.0), 8, axis=1)[..., None]
    return vals.transpose(0, 1, 3, 2).reshape(g * 512, n)


E2M1 = np.array([0.0, 0.5, 1.0, 1.5, 2.0, 3.0, 4.0, 6.0, -0.0, -0.5, -1.0, -1.5, -2.0, -3.0, -4.0, -6.0])


def pack_fp4(w):
    k, n = w.shape
    w = f64(np.asarray(w, np.float32).astype(ml_dtypes.bfloat16)).reshape(k // 32, 32, n)
    amax = np.abs(w).max(1)
    mant, ex = np.frexp(amax / 6.0)
    byte = np.clip(np.where(amax > 0, np.where(mant > 0.5, ex, ex - 1) + 127, 1), 1, 254)
    scaled = (w * np.exp2(127.0 - byte)[:, None, :]).reshape(k, n).astype(np.float32)
    c = np.ascontiguousarray(scaled.reshape(k // 512, 128, 4, n).transpose(0, 1, 3, 2)).astype(ml_dtypes.float4_e2m1fn).view(np.uint8) & 0xF
    words = (c[..., 0::2] | (c[..., 1::2] << 4)).reshape(k // 512, 128, 2 * n)
    return np.ascontiguousarray(words), np.ascontiguousarray(byte.astype(np.uint8).reshape(k // 512, 16, n))


def unpack_fp4(words, scales):
    g, _, n = scales.shape
    words = np.ascontiguousarray(words).reshape(g, 128, n, 2)
    nib = np.empty((g, 128, n, 4), np.uint8)
    nib[..., 0::2] = words & 0xF
    nib[..., 1::2] = words >> 4
    vals = E2M1[nib] * np.repeat(np.exp2(scales.astype(np.float64) - 127.0), 8, axis=1)[..., None]
    return vals.transpose(0, 1, 3, 2).reshape(g * 512, n)


def relu(v):
    return np.maximum(v, 0.0)


K, T, S, N, H = 512, 1024, 512, 256, 512


def setup_inputs():
    n = np.random.standard_normal
    s = mx_kscale(K)[:, None]
    u = mx_kscale(H)
    packed_xT = pack_weight(n((K, T)) * s)
    packed_w1 = pack_fp4(n((K, H)) / np.sqrt(K) / s)
    packed_w2 = pack_fp4(n((H, N)) / np.sqrt(H) / u[:, None])
    return {
        "x_words": packed_xT[0],
        "x_scales": packed_xT[1],
        "w1_words": packed_w1[0],
        "w1_scales": packed_w1[1],
        "alp": (np.random.uniform(0.15, 0.4, (H, S))).astype(np.float32),
        "unit": (np.random.uniform(0.6, 1.4, (H, 1)) * u[:, None]).astype(np.float32),
        "w2_words": packed_w2[0],
        "w2_scales": packed_w2[1],
        "offs": striped(np.random.permutation(T)[:S]),
        "in1": striped(np.random.permutation(S)),
        "in2": striped(np.random.permutation(S)),
    }


def reference(x_words, x_scales, w1_words, w1_scales, alp, unit, w2_words, w2_scales, offs, in1, in2):
    xq = unpack_weight(x_words, x_scales)[:, unstriped(offs)]
    y = unpack_fp4(w1_words, w1_scales).T @ xq
    res = np.abs(y)
    est = f64(alp) * res
    snd = (-1.0 * f64(alp) + 1.0) * res
    s1 = snd[:, unstriped(in1)]
    s2 = snd[:, unstriped(in2)]
    res2 = 0.5 * (s1 + s2)
    hot = relu(res2 - 0.5)
    est2 = est + f64(alp) * hot
    hid = f64(unit) * (est2 * (np.log(res2[:, unstriped(in2)] + 0.3)))
    return unpack_fp4(w2_words, w2_scales).T @ mxq(hid, 0, "e4m3")

@@ -1,0 +1,181 @@
+from contextlib import ExitStack
+
+import concourse.mybir as mybir
+
+K, T, S, N, H = 512, 1024, 512, 256, 512
+FLOPS = 2 * K * H * S + 2 * H * N * S
+
+F32 = mybir.dt.float32
+BF16 = mybir.dt.bfloat16
+I32 = mybir.dt.int32
+U32 = mybir.dt.uint32
+U16 = mybir.dt.uint16
+U8 = mybir.dt.uint8
+FP8X4 = mybir.dt.float8_e4m3fn_x4
+FP4X4 = mybir.dt.float4_e2m1fn_x4
+ALU = mybir.AluOpType
+ACT = mybir.ActivationFunctionType
+
+P = 128
+PACK = 4
+PIECES = 2
+W = S // PIECES
+
+
+def load_scale_rows(queue, plane, rows):
+    for q in range(4):
+        queue.dma_start(out=plane[32 * q : 32 * q + 4, :].bitcast(I32), in_=rows[4 * q : 4 * q + 4, :].bitcast(I32))
+
+
+def tile_picked_ypushpr_log_p_kernel(
+    tc, x_words, x_scales, w1_words, w1_scales, alp, unit, w2_words, w2_scales, offs, in1, in2, out
+):
+    nc = tc.nc
+    with ExitStack() as ctx:
+        keep = ctx.enter_context(tc.tile_pool(name="keep", bufs=1))
+        psum = ctx.enter_context(tc.psum_pool(name="psum", bufs=1))
+
+        offs_sb = keep.tile([P, S // 16], U16, name="offs_sb")
+        in1_sb = keep.tile([P, S // 16], U16, name="in1_sb")
+        in2_sb = keep.tile([P, S // 16], U16, name="in2_sb")
+        xw = keep.tile([P, T], U32, name="xw", align_bytes=64)
+        xs = keep.tile([P, T], U8, name="xs", align_bytes=64)
+        w1w_raw = keep.tile([P, 2 * H], U8, name="w1w_raw", align_bytes=64)
+        w1s_raw = keep.tile([P, H], U8, name="w1s_raw", align_bytes=64)
+        w2w = keep.tile([P, 2 * N], U8, name="w2w", align_bytes=64)
+        w2s = keep.tile([P, N], U8, name="w2s", align_bytes=64)
+        unit_sb = keep.tile([P, PACK], F32, name="unit_sb")
+        alp_sb = [keep.tile([P, S], F32, name=f"alp{t}", align_bytes=64) for t in range(PACK)]
+
+        nc.vector.memset(xs[:].bitcast(I32), 0)
+        nc.gpsimd.memset(w1s_raw[:].bitcast(I32), 0)
+        nc.gpsimd.memset(w2s[:].bitcast(I32), 0)
+
+        alp_v = alp.rearrange("(p t) j -> p t j", t=PACK)
+        nc.sync.dma_start(out=xw[:].bitcast(I32), in_=x_words[0].rearrange("p n r -> p (n r)").bitcast(I32))
+        load_scale_rows(nc.sync, xs, x_scales[0])
+        nc.sync.dma_start(offs_sb[:], offs)
+        nc.sync.dma_start(out=w1w_raw[:].bitcast(I32), in_=w1_words[0].bitcast(I32))
+        load_scale_rows(nc.sync, w1s_raw, w1_scales[0])
+        nc.sync.dma_start(out=alp_sb[0][:], in_=alp_v[:, 0, :])
+        nc.sync.dma_start(in1_sb[:], in1)
+        nc.sync.dma_start(out=alp_sb[1][:], in_=alp_v[:, 1, :])
+        nc.sync.dma_start(in2_sb[:], in2)
+        nc.sync.dma_start(out=alp_sb[2][:], in_=alp_v[:, 2, :])
+        nc.sync.dma_start(out=alp_sb[3][:], in_=alp_v[:, 3, :])
+        nc.sync.dma_start(out=unit_sb[:], in_=unit.rearrange("(p t) o -> p (t o)", t=PACK))
+        nc.sync.dma_start(out=w2w[:].bitcast(I32), in_=w2_words[0].bitcast(I32))
+        load_scale_rows(nc.sync, w2s, w2_scales[0])
+
+        xw_g = keep.tile([P, S], U32, name="xw_g", align_bytes=64)
+        xs_g = keep.tile([P, S], U8, name="xs_g", align_bytes=64)
+        nc.vector.tensor_copy(xs_g[:], xs[:].indirect(offs_sb[:]))
+        nc.vector.tensor_copy(xw_g[:], xw[:].indirect(offs_sb[:]))
+
+        w1w = keep.tile([P, PACK, 2 * P], U8, name="w1w", align_bytes=64)
+        w1s = keep.tile([P, PACK, P], U8, name="w1s", align_bytes=64)
+        w1w_src = w1w_raw[:].rearrange("p (m t b) -> p t m b", t=PACK, b=2)
+        w1s_src = w1s_raw[:].rearrange("p (m t) -> p t m", t=PACK)
+        w1w_dst = w1w[:].rearrange("p t (m b) -> p t m b", b=2)
+
+        def deal(lo, hi):
+            nc.vector.tensor_copy(w1w_dst[:, lo:hi], w1w_src[:, lo:hi])
+            nc.vector.tensor_copy(w1s[:, lo:hi], w1s_src[:, lo:hi])
+
+        y = [psum.tile([P, S], F32, name=f"y{t}") for t in range(PACK)]
+        win_a = [keep.tile([P, 2 * S], F32, name=f"win_a{t}", align_bytes=64) for t in range(PACK)]
+        win_b = [keep.tile([P, 2 * S], F32, name=f"win_b{t}", align_bytes=64) for t in range(PACK)]
+        share = [keep.tile([P, S], F32, name=f"share{t}", align_bytes=64) for t in range(PACK)]
+        first = [keep.tile([P, S], F32, name=f"first{t}", align_bytes=64) for t in range(PACK)]
+        mass = [keep.tile([P, S], F32, name=f"mass{t}", align_bytes=64) for t in range(PACK)]
+        est = keep.tile([P, PACK, S], F32, name="est", align_bytes=64)
+        logg = keep.tile([P, PACK, S], F32, name="logg", align_bytes=64)
+
+        def product(t):
+            nc.tensor.matmul_mx(y[t][:], lhsT=w1w[:, t, :].bitcast(FP4X4), lhsT_scale=w1s[:, t, :],
+                                rhs=xw_g[:].bitcast(FP8X4), rhs_scale=xs_g[:], start=True, stop=True)
+
+        def absval(t):
+            nc.scalar.activation(win_a[t][:, S:], y[t][:], ACT.Abs)
+
+        def send(t):
+            nc.vector.tensor_scalar(share[t][:], alp_sb[t][:], -0.5, 0.5, ALU.mult, ALU.add)
+            nc.vector.tensor_tensor(win_a[t][:, :S], win_a[t][:, S:], share[t][:], ALU.mult)
+
+        def fetch1(t):
+            nc.scalar.activation(first[t][:], win_a[t][:].indirect(in1_sb[:]), ACT.Copy, bias=-0.5)
+
+        def fetch2(t):
+            nc.vector.tensor_tensor(win_b[t][:, S:], win_a[t][:].indirect(in2_sb[:]), first[t][:], ALU.add)
+
+        def logv(t):
+            nc.scalar.activation(win_b[t][:, :S], win_b[t][:, S:], ACT.Ln, bias=0.8)
+
+        def massv(t):
+            nc.vector.scalar_tensor_tensor(mass[t][:], win_b[t][:, S:], 0.0, win_a[t][:, S:], ALU.max, ALU.add)
+
+        def estv(t):
+            nc.vector.scalar_tensor_tensor(est[:, t, :], mass[t][:], unit_sb[:, t : t + 1], alp_sb[t][:], ALU.mult, ALU.mult)
+
+        def fetch3(t, lo, hi):
+            nc.scalar.activation(logg[:, t, lo:hi], win_b[t][:].indirect(in2_sb[:, lo // 16 : hi // 16]), ACT.Copy)
+
+        deal(0, 1)
+        product(0)
+        deal(1, PACK)
+        for t in range(1, PACK):
+            product(t)
+        absval(0)
+        send(0)
+        absval(1)
+        send(1)
+        fetch1(0)
+        fetch2(0)
+        absval(2)
+        send(2)
+        fetch1(1)
+        logv(0)
+        massv(0)
+        fetch2(1)
+        estv(0)
+        absval(3)
+        send(3)
+        fetch1(2)
+        massv(1)
+        fetch3(0, 0, S)
+        fetch2(2)
+        logv(1)
+        estv(1)
+        fetch1(3)
+        fetch2(3)
+        fetch3(1, 0, S)
+        logv(2)
+        massv(2)
+        massv(3)
+        fetch3(2, 0, S)
+        estv(2)
+        estv(3)
+        logv(3)
+        out_v = out.rearrange("(b p) j -> p b j", p=P)
+        for c in range(PIECES):
+            fetch3(3, c * W, (c + 1) * W)
+        for c in range(PIECES):
+            cols = slice(c * W, (c + 1) * W)
+            hid = keep.tile([P, W * PACK], BF16, name=f"hid{c}", align_bytes=64)
+            nc.vector.tensor_tensor(
+                hid[:].rearrange("p (c i t) -> p c t i", i=4, t=PACK),
+                logg[:, :, cols].rearrange("p t (c i) -> p c t i", i=4),
+                est[:, :, cols].rearrange("p t (c i) -> p c t i", i=4),
+                ALU.mult,
+            )
+            hw = keep.tile([P, W], U32, name=f"hw{c}", align_bytes=64)
+            hs = keep.tile([P, W], U8, name=f"hs{c}", align_bytes=64)
+            nc.vector.quantize_mx(out=hw[:].bitcast(FP8X4), scales=hs[:], in_=hid[:])
+            acc = psum.tile([P, N // P, W], F32, name=f"acc{c}")
+            for b in range(N // P):
+                nc.tensor.matmul_mx(acc[:, b, :], lhsT=w2w[:, 2 * P * b : 2 * P * (b + 1)].bitcast(FP4X4),
+                                    lhsT_scale=w2s[:, P * b : P * (b + 1)],
+                                    rhs=hw[:].bitcast(FP8X4), rhs_scale=hs[:], start=True, stop=True)
+            res_sb = keep.tile([P, N // P, W], F32, name=f"res_sb{c}", align_bytes=64)
+            nc.scalar.activation(res_sb[:], acc[:], ACT.Copy)
+            nc.sync.dma_start(out=out_v[:, :, cols], in_=res_sb[:])

@@ -18,7 +18,7 @@ ACT = mybir.ActivationFunctionType
 
 P = 128
 PACK = 4
-PIECES = 2
+PIECES = 4
 W = S // PIECES
 
 
@@ -45,24 +45,26 @@ def tile_picked_ypushpr_log_p_kernel(
         w2w = keep.tile([P, 2 * N], U8, name="w2w", align_bytes=64)
         w2s = keep.tile([P, N], U8, name="w2s", align_bytes=64)
         unit_sb = keep.tile([P, PACK], F32, name="unit_sb")
-        alp_sb = [keep.tile([P, S], F32, name=f"alp{t}", align_bytes=64) for t in range(PACK)]
+        alp_two = [keep.tile([P, 2, S], F32, name=f"alp{u}", align_bytes=64) for u in range(2)]
+        alp_sb = [alp_two[t // 2][:, t % 2, :] for t in range(PACK)]
 
-        nc.vector.memset(xs[:].bitcast(I32), 0)
+        nc.gpsimd.memset(xs[:].bitcast(I32), 0)
         nc.gpsimd.memset(w1s_raw[:].bitcast(I32), 0)
-        nc.gpsimd.memset(w2s[:].bitcast(I32), 0)
+        nc.vector.memset(w2s[:].bitcast(I32), 0)
+        warm = keep.tile([P, 2], F32, name="warm")
+        nc.vector.memset(warm[:, 0:1], 1.0)
+        nc.scalar.activation(warm[:, 1:2], warm[:, 0:1], ACT.Ln)
 
         alp_v = alp.rearrange("(p t) j -> p t j", t=PACK)
-        nc.sync.dma_start(out=xw[:].bitcast(I32), in_=x_words[0].rearrange("p n r -> p (n r)").bitcast(I32))
-        load_scale_rows(nc.sync, xs, x_scales[0])
-        nc.sync.dma_start(offs_sb[:], offs)
         nc.sync.dma_start(out=w1w_raw[:].bitcast(I32), in_=w1_words[0].bitcast(I32))
+        nc.sync.dma_start(offs_sb[:], offs)
+        load_scale_rows(nc.sync, xs, x_scales[0])
+        nc.sync.dma_start(out=xw[:].bitcast(I32), in_=x_words[0].rearrange("p n r -> p (n r)").bitcast(I32))
         load_scale_rows(nc.sync, w1s_raw, w1_scales[0])
-        nc.sync.dma_start(out=alp_sb[0][:], in_=alp_v[:, 0, :])
+        nc.sync.dma_start(out=alp_two[0][:], in_=alp_v[:, 0:2, :])
         nc.sync.dma_start(in1_sb[:], in1)
-        nc.sync.dma_start(out=alp_sb[1][:], in_=alp_v[:, 1, :])
+        nc.sync.dma_start(out=alp_two[1][:], in_=alp_v[:, 2:4, :])
         nc.sync.dma_start(in2_sb[:], in2)
-        nc.sync.dma_start(out=alp_sb[2][:], in_=alp_v[:, 2, :])
-        nc.sync.dma_start(out=alp_sb[3][:], in_=alp_v[:, 3, :])
         nc.sync.dma_start(out=unit_sb[:], in_=unit.rearrange("(p t) o -> p (t o)", t=PACK))
         nc.sync.dma_start(out=w2w[:].bitcast(I32), in_=w2_words[0].bitcast(I32))
         load_scale_rows(nc.sync, w2s, w2_scales[0])
@@ -84,8 +86,8 @@ def tile_picked_ypushpr_log_p_kernel(
 
         y = [psum.tile([P, S], F32, name=f"y{t}") for t in range(PACK)]
         win_a = [keep.tile([P, 2 * S], F32, name=f"win_a{t}", align_bytes=64) for t in range(PACK)]
-        win_b = [keep.tile([P, 2 * S], F32, name=f"win_b{t}", align_bytes=64) for t in range(PACK)]
-        share = [keep.tile([P, S], F32, name=f"share{t}", align_bytes=64) for t in range(PACK)]
+        over = [keep.tile([P, S], F32, name=f"over{t}", align_bytes=64) for t in range(PACK)]
+        logs = {}
         first = [keep.tile([P, S], F32, name=f"first{t}", align_bytes=64) for t in range(PACK)]
         mass = [keep.tile([P, S], F32, name=f"mass{t}", align_bytes=64) for t in range(PACK)]
         est = keep.tile([P, PACK, S], F32, name="est", align_bytes=64)
@@ -99,26 +101,29 @@ def tile_picked_ypushpr_log_p_kernel(
             nc.scalar.activation(win_a[t][:, S:], y[t][:], ACT.Abs)
 
         def send(t):
-            nc.vector.tensor_scalar(share[t][:], alp_sb[t][:], -0.5, 0.5, ALU.mult, ALU.add)
-            nc.vector.tensor_tensor(win_a[t][:, :S], win_a[t][:, S:], share[t][:], ALU.mult)
+            share = keep.tile([P, S], F32, name=f"share{t}", tag=f"turn{t % 2}", align_bytes=64)
+            nc.vector.tensor_scalar(share[:], alp_sb[t], -0.5, 0.5, ALU.mult, ALU.add)
+            nc.vector.tensor_tensor(win_a[t][:, :S], win_a[t][:, S:], share[:], ALU.mult)
 
         def fetch1(t):
             nc.scalar.activation(first[t][:], win_a[t][:].indirect(in1_sb[:]), ACT.Copy, bias=-0.5)
 
         def fetch2(t):
-            nc.vector.tensor_tensor(win_b[t][:, S:], win_a[t][:].indirect(in2_sb[:]), first[t][:], ALU.add)
+            nc.vector.tensor_tensor(over[t][:], win_a[t][:].indirect(in2_sb[:]), first[t][:], ALU.add)
 
         def logv(t):
-            nc.scalar.activation(win_b[t][:, :S], win_b[t][:, S:], ACT.Ln, bias=0.8)
+            tag = "turn1" if t == 0 else f"log{t}"
+            logs[t] = keep.tile([P, S], F32, name=f"log{t}", tag=tag, align_bytes=64)
+            nc.scalar.activation(logs[t][:], over[t][:], ACT.Ln, bias=0.8)
 
         def massv(t):
-            nc.vector.scalar_tensor_tensor(mass[t][:], win_b[t][:, S:], 0.0, win_a[t][:, S:], ALU.max, ALU.add)
+            nc.vector.scalar_tensor_tensor(mass[t][:], over[t][:], 0.0, win_a[t][:, S:], ALU.max, ALU.add)
 
         def estv(t):
-            nc.vector.scalar_tensor_tensor(est[:, t, :], mass[t][:], unit_sb[:, t : t + 1], alp_sb[t][:], ALU.mult, ALU.mult)
+            nc.vector.scalar_tensor_tensor(est[:, t, :], mass[t][:], unit_sb[:, t : t + 1], alp_sb[t], ALU.mult, ALU.mult)
 
         def fetch3(t, lo, hi):
-            nc.scalar.activation(logg[:, t, lo:hi], win_b[t][:].indirect(in2_sb[:, lo // 16 : hi // 16]), ACT.Copy)
+            nc.scalar.activation(logg[:, t, lo:hi], logs[t][:].indirect(in2_sb[:, lo // 16 : hi // 16]), ACT.Copy)
 
         deal(0, 1)
         product(0)
@@ -127,38 +132,20 @@ def tile_picked_ypushpr_log_p_kernel(
             product(t)
         absval(0)
         send(0)
-        absval(1)
-        send(1)
-        fetch1(0)
-        fetch2(0)
-        absval(2)
-        send(2)
-        fetch1(1)
-        logv(0)
-        massv(0)
-        fetch2(1)
-        estv(0)
-        absval(3)
-        send(3)
-        fetch1(2)
-        massv(1)
-        fetch3(0, 0, S)
-        fetch2(2)
-        logv(1)
-        estv(1)
-        fetch1(3)
-        fetch2(3)
-        fetch3(1, 0, S)
-        logv(2)
-        massv(2)
-        massv(3)
-        fetch3(2, 0, S)
-        estv(2)
-        estv(3)
-        logv(3)
+        for t in range(PACK):
+            if t + 1 < PACK:
+                absval(t + 1)
+                send(t + 1)
+            fetch1(t)
+            fetch2(t)
+        for t in range(PACK):
+            logv(t)
+            massv(t)
+            estv(t)
         out_v = out.rearrange("(b p) j -> p b j", p=P)
-        for c in range(PIECES):
-            fetch3(3, c * W, (c + 1) * W)
+        for h in range(2):
+            for t in range(PACK):
+                fetch3(t, h * S // 2, (h + 1) * S // 2)
         for c in range(PIECES):
             cols = slice(c * W, (c + 1) * W)
             hid = keep.tile([P, W * PACK], BF16, name=f"hid{c}", align_bytes=64)

@@ -45,8 +45,8 @@ def tile_picked_ypushpr_log_p_kernel(
         w2w = keep.tile([P, 2 * N], U8, name="w2w", align_bytes=64)
         w2s = keep.tile([P, N], U8, name="w2s", align_bytes=64)
         unit_sb = keep.tile([P, PACK], F32, name="unit_sb")
-        alp_two = [keep.tile([P, 2, S], F32, name=f"alp{u}", align_bytes=64) for u in range(2)]
-        alp_sb = [alp_two[t // 2][:, t % 2, :] for t in range(PACK)]
+        alp_all = keep.tile([P, PACK, S], F32, name="alp_all", align_bytes=64)
+        alp_sb = [alp_all[:, t, :] for t in range(PACK)]
 
         nc.gpsimd.memset(xs[:].bitcast(I32), 0)
         nc.gpsimd.memset(w1s_raw[:].bitcast(I32), 0)
@@ -60,10 +60,10 @@ def tile_picked_ypushpr_log_p_kernel(
         nc.sync.dma_start(offs_sb[:], offs)
         load_scale_rows(nc.sync, xs, x_scales[0])
         nc.sync.dma_start(out=xw[:].bitcast(I32), in_=x_words[0].rearrange("p n r -> p (n r)").bitcast(I32))
+        nc.sync.dma_start(out=alp_all[:, 0:2, :], in_=alp_v[:, 0:2, :])
         load_scale_rows(nc.sync, w1s_raw, w1_scales[0])
-        nc.sync.dma_start(out=alp_two[0][:], in_=alp_v[:, 0:2, :])
+        nc.sync.dma_start(out=alp_all[:, 2:4, :], in_=alp_v[:, 2:4, :])
         nc.sync.dma_start(in1_sb[:], in1)
-        nc.sync.dma_start(out=alp_two[1][:], in_=alp_v[:, 2:4, :])
         nc.sync.dma_start(in2_sb[:], in2)
         nc.sync.dma_start(out=unit_sb[:], in_=unit.rearrange("(p t) o -> p (t o)", t=PACK))
         nc.sync.dma_start(out=w2w[:].bitcast(I32), in_=w2_words[0].bitcast(I32))
@@ -71,8 +71,15 @@ def tile_picked_ypushpr_log_p_kernel(
 
         xw_g = keep.tile([P, S], U32, name="xw_g", align_bytes=64)
         xs_g = keep.tile([P, S], U8, name="xs_g", align_bytes=64)
-        nc.vector.tensor_copy(xs_g[:], xs[:].indirect(offs_sb[:]))
-        nc.vector.tensor_copy(xw_g[:], xw[:].indirect(offs_sb[:]))
+        halves = [slice(0, S // 2), slice(S // 2, S)]
+        whole = [slice(0, S)]
+
+        def entries(lst, cols):
+            return lst[:, cols.start // 16 : cols.stop // 16]
+
+        for cols in halves:
+            nc.vector.tensor_copy(xs_g[:, cols], xs[:].indirect(entries(offs_sb, cols)))
+            nc.vector.tensor_copy(xw_g[:, cols], xw[:].indirect(entries(offs_sb, cols)))
 
         w1w = keep.tile([P, PACK, 2 * P], U8, name="w1w", align_bytes=64)
         w1s = keep.tile([P, PACK, P], U8, name="w1s", align_bytes=64)
@@ -84,35 +91,49 @@ def tile_picked_ypushpr_log_p_kernel(
             nc.vector.tensor_copy(w1w_dst[:, lo:hi], w1w_src[:, lo:hi])
             nc.vector.tensor_copy(w1s[:, lo:hi], w1s_src[:, lo:hi])
 
-        y = [psum.tile([P, S], F32, name=f"y{t}") for t in range(PACK)]
         win_a = [keep.tile([P, 2 * S], F32, name=f"win_a{t}", align_bytes=64) for t in range(PACK)]
         over = [keep.tile([P, S], F32, name=f"over{t}", align_bytes=64) for t in range(PACK)]
         logs = {}
+        y = {}
+        share_a = keep.tile([P, 2, S], F32, name="share_a", align_bytes=64)
+        share_b = keep.tile([P, 2, S], F32, name="share_b", tag="share_b", align_bytes=64)
+        share = [(share_a, share_b)[t // 2][:, t % 2, :] for t in range(PACK)]
         first = [keep.tile([P, S], F32, name=f"first{t}", align_bytes=64) for t in range(PACK)]
         mass = [keep.tile([P, S], F32, name=f"mass{t}", align_bytes=64) for t in range(PACK)]
         est = keep.tile([P, PACK, S], F32, name="est", align_bytes=64)
         logg = keep.tile([P, PACK, S], F32, name="logg", align_bytes=64)
 
+        def cuts(t):
+            return halves if t == 0 else whole
+
         def product(t):
-            nc.tensor.matmul_mx(y[t][:], lhsT=w1w[:, t, :].bitcast(FP4X4), lhsT_scale=w1s[:, t, :],
-                                rhs=xw_g[:].bitcast(FP8X4), rhs_scale=xs_g[:], start=True, stop=True)
+            for cols in cuts(t):
+                y[t, cols.start] = psum.tile([P, cols.stop - cols.start], F32, name=f"y{t}_{cols.start}", tag=f"bank{t}_{cols.start}")
+                nc.tensor.matmul_mx(y[t, cols.start][:], lhsT=w1w[:, t, :].bitcast(FP4X4), lhsT_scale=w1s[:, t, :],
+                                    rhs=xw_g[:, cols].bitcast(FP8X4), rhs_scale=xs_g[:, cols], start=True, stop=True)
 
         def absval(t):
-            nc.scalar.activation(win_a[t][:, S:], y[t][:], ACT.Abs)
+            for cols in cuts(t):
+                nc.scalar.activation(win_a[t][:, S + cols.start : S + cols.stop], y[t, cols.start][:], ACT.Abs)
 
         def send(t):
-            share = keep.tile([P, S], F32, name=f"share{t}", tag=f"turn{t % 2}", align_bytes=64)
-            nc.vector.tensor_scalar(share[:], alp_sb[t], -0.5, 0.5, ALU.mult, ALU.add)
-            nc.vector.tensor_tensor(win_a[t][:, :S], win_a[t][:, S:], share[:], ALU.mult)
+            if t < 2:
+                nc.scalar.activation(share[t], alp_sb[t], ACT.Copy, scale=-0.5, bias=0.5)
+            elif t == 2:
+                nc.vector.tensor_scalar(share_b[:], alp_all[:, 2:4, :], -0.5, 0.5, ALU.mult, ALU.add)
+            for cols in cuts(t):
+                nc.vector.tensor_tensor(win_a[t][:, cols], win_a[t][:, S + cols.start : S + cols.stop], share[t][:, cols], ALU.mult)
 
         def fetch1(t):
-            nc.scalar.activation(first[t][:], win_a[t][:].indirect(in1_sb[:]), ACT.Copy, bias=-0.5)
+            for cols in cuts(t):
+                nc.scalar.activation(first[t][:, cols], win_a[t][:].indirect(entries(in1_sb, cols)), ACT.Copy, bias=-0.5)
 
         def fetch2(t):
-            nc.vector.tensor_tensor(over[t][:], win_a[t][:].indirect(in2_sb[:]), first[t][:], ALU.add)
+            for cols in cuts(t):
+                nc.vector.tensor_tensor(over[t][:, cols], win_a[t][:].indirect(entries(in2_sb, cols)), first[t][:, cols], ALU.add)
 
         def logv(t):
-            tag = "turn1" if t == 0 else f"log{t}"
+            tag = "share_b" if t == 0 else f"log{t}"
             logs[t] = keep.tile([P, S], F32, name=f"log{t}", tag=tag, align_bytes=64)
             nc.scalar.activation(logs[t][:], over[t][:], ACT.Ln, bias=0.8)
 
@@ -158,11 +179,20 @@ def tile_picked_ypushpr_log_p_kernel(
             hw = keep.tile([P, W], U32, name=f"hw{c}", align_bytes=64)
             hs = keep.tile([P, W], U8, name=f"hs{c}", align_bytes=64)
             nc.vector.quantize_mx(out=hw[:].bitcast(FP8X4), scales=hs[:], in_=hid[:])
-            acc = psum.tile([P, N // P, W], F32, name=f"acc{c}")
+            res_sb = keep.tile([P, N // P, W], F32, name=f"res_sb{c}", align_bytes=64)
+            last = c == PIECES - 1
+            if last:
+                acc = [psum.tile([P, W], F32, name=f"acc{c}_{b}", tag=f"bank_last{b}")[:] for b in range(N // P)]
+            else:
+                both = psum.tile([P, N // P, W], F32, name=f"acc{c}", tag=f"bank{c}_0")
+                acc = [both[:, b, :] for b in range(N // P)]
             for b in range(N // P):
-                nc.tensor.matmul_mx(acc[:, b, :], lhsT=w2w[:, 2 * P * b : 2 * P * (b + 1)].bitcast(FP4X4),
+                nc.tensor.matmul_mx(acc[b], lhsT=w2w[:, 2 * P * b : 2 * P * (b + 1)].bitcast(FP4X4),
                                     lhsT_scale=w2s[:, P * b : P * (b + 1)],
                                     rhs=hw[:].bitcast(FP8X4), rhs_scale=hs[:], start=True, stop=True)
-            res_sb = keep.tile([P, N // P, W], F32, name=f"res_sb{c}", align_bytes=64)
-            nc.scalar.activation(res_sb[:], acc[:], ACT.Copy)
+            if last:
+                nc.scalar.activation(res_sb[:, 0, :], acc[0], ACT.Copy)
+                nc.vector.tensor_copy(res_sb[:, 1, :], acc[1])
+            else:
+                nc.scalar.activation(res_sb[:], both[:], ACT.Copy)
             nc.sync.dma_start(out=out_v[:, :, cols], in_=res_sb[:])

from contextlib import ExitStack

import concourse.mybir as mybir

K, T, S, N, H = 512, 1024, 512, 256, 512
FLOPS = 2 * K * H * S + 2 * H * N * S

F32 = mybir.dt.float32
BF16 = mybir.dt.bfloat16
I32 = mybir.dt.int32
U32 = mybir.dt.uint32
U16 = mybir.dt.uint16
U8 = mybir.dt.uint8
FP8X4 = mybir.dt.float8_e4m3fn_x4
FP4X4 = mybir.dt.float4_e2m1fn_x4
ALU = mybir.AluOpType
ACT = mybir.ActivationFunctionType

P = 128
PACK = 4
PIECES = 4
W = S // PIECES


def load_scale_rows(queue, plane, rows):
    for q in range(4):
        queue.dma_start(out=plane[32 * q : 32 * q + 4, :].bitcast(I32), in_=rows[4 * q : 4 * q + 4, :].bitcast(I32))


def tile_picked_ypushpr_log_p_kernel(
    tc, x_words, x_scales, w1_words, w1_scales, alp, unit, w2_words, w2_scales, offs, in1, in2, out
):
    nc = tc.nc
    with ExitStack() as ctx:
        keep = ctx.enter_context(tc.tile_pool(name="keep", bufs=1))
        psum = ctx.enter_context(tc.psum_pool(name="psum", bufs=1))

        offs_sb = keep.tile([P, S // 16], U16, name="offs_sb")
        in1_sb = keep.tile([P, S // 16], U16, name="in1_sb")
        in2_sb = keep.tile([P, S // 16], U16, name="in2_sb")
        xw = keep.tile([P, T], U32, name="xw", align_bytes=64)
        xs = keep.tile([P, T], U8, name="xs", align_bytes=64)
        w1w_raw = keep.tile([P, 2 * H], U8, name="w1w_raw", align_bytes=64)
        w1s_raw = keep.tile([P, H], U8, name="w1s_raw", align_bytes=64)
        w2w = keep.tile([P, 2 * N], U8, name="w2w", align_bytes=64)
        w2s = keep.tile([P, N], U8, name="w2s", align_bytes=64)
        unit_sb = keep.tile([P, PACK], F32, name="unit_sb")
        alp_all = keep.tile([P, PACK, S], F32, name="alp_all", align_bytes=64)
        alp_sb = [alp_all[:, t, :] for t in range(PACK)]

        nc.gpsimd.memset(xs[:].bitcast(I32), 0)
        nc.gpsimd.memset(w1s_raw[:].bitcast(I32), 0)
        nc.vector.memset(w2s[:].bitcast(I32), 0)
        warm = keep.tile([P, 2], F32, name="warm")
        nc.vector.memset(warm[:, 0:1], 1.0)
        nc.scalar.activation(warm[:, 1:2], warm[:, 0:1], ACT.Ln)

        alp_v = alp.rearrange("(p t) j -> p t j", t=PACK)
        nc.sync.dma_start(out=w1w_raw[:].bitcast(I32), in_=w1_words[0].bitcast(I32))
        nc.sync.dma_start(offs_sb[:], offs)
        load_scale_rows(nc.sync, xs, x_scales[0])
        nc.sync.dma_start(out=xw[:].bitcast(I32), in_=x_words[0].rearrange("p n r -> p (n r)").bitcast(I32))
        nc.sync.dma_start(out=alp_all[:, 0:2, :], in_=alp_v[:, 0:2, :])
        load_scale_rows(nc.sync, w1s_raw, w1_scales[0])
        nc.sync.dma_start(out=alp_all[:, 2:4, :], in_=alp_v[:, 2:4, :])
        nc.sync.dma_start(in1_sb[:], in1)
        nc.sync.dma_start(in2_sb[:], in2)
        nc.sync.dma_start(out=unit_sb[:], in_=unit.rearrange("(p t) o -> p (t o)", t=PACK))
        nc.sync.dma_start(out=w2w[:].bitcast(I32), in_=w2_words[0].bitcast(I32))
        load_scale_rows(nc.sync, w2s, w2_scales[0])

        xw_g = keep.tile([P, S], U32, name="xw_g", align_bytes=64)
        xs_g = keep.tile([P, S], U8, name="xs_g", align_bytes=64)
        halves = [slice(0, S // 2), slice(S // 2, S)]
        whole = [slice(0, S)]

        def entries(lst, cols):
            return lst[:, cols.start // 16 : cols.stop // 16]

        for cols in halves:
            nc.vector.tensor_copy(xs_g[:, cols], xs[:].indirect(entries(offs_sb, cols)))
            nc.vector.tensor_copy(xw_g[:, cols], xw[:].indirect(entries(offs_sb, cols)))

        w1w = keep.tile([P, PACK, 2 * P], U8, name="w1w", align_bytes=64)
        w1s = keep.tile([P, PACK, P], U8, name="w1s", align_bytes=64)
        w1w_src = w1w_raw[:].rearrange("p (m t b) -> p t m b", t=PACK, b=2)
        w1s_src = w1s_raw[:].rearrange("p (m t) -> p t m", t=PACK)
        w1w_dst = w1w[:].rearrange("p t (m b) -> p t m b", b=2)

        def deal(lo, hi):
            nc.vector.tensor_copy(w1w_dst[:, lo:hi], w1w_src[:, lo:hi])
            nc.vector.tensor_copy(w1s[:, lo:hi], w1s_src[:, lo:hi])

        win_a = [keep.tile([P, 2 * S], F32, name=f"win_a{t}", align_bytes=64) for t in range(PACK)]
        over = [keep.tile([P, S], F32, name=f"over{t}", align_bytes=64) for t in range(PACK)]
        logs = {}
        y = {}
        share_a = keep.tile([P, 2, S], F32, name="share_a", align_bytes=64)
        share_b = keep.tile([P, 2, S], F32, name="share_b", tag="share_b", align_bytes=64)
        share = [(share_a, share_b)[t // 2][:, t % 2, :] for t in range(PACK)]
        first = [keep.tile([P, S], F32, name=f"first{t}", align_bytes=64) for t in range(PACK)]
        mass = [keep.tile([P, S], F32, name=f"mass{t}", align_bytes=64) for t in range(PACK)]
        est = keep.tile([P, PACK, S], F32, name="est", align_bytes=64)
        logg = keep.tile([P, PACK, S], F32, name="logg", align_bytes=64)

        def cuts(t):
            return halves if t == 0 else whole

        def product(t):
            for cols in cuts(t):
                y[t, cols.start] = psum.tile([P, cols.stop - cols.start], F32, name=f"y{t}_{cols.start}", tag=f"bank{t}_{cols.start}")
                nc.tensor.matmul_mx(y[t, cols.start][:], lhsT=w1w[:, t, :].bitcast(FP4X4), lhsT_scale=w1s[:, t, :],
                                    rhs=xw_g[:, cols].bitcast(FP8X4), rhs_scale=xs_g[:, cols], start=True, stop=True)

        def absval(t):
            for cols in cuts(t):
                nc.scalar.activation(win_a[t][:, S + cols.start : S + cols.stop], y[t, cols.start][:], ACT.Abs)

        def send(t):
            if t < 2:
                nc.scalar.activation(share[t], alp_sb[t], ACT.Copy, scale=-0.5, bias=0.5)
            elif t == 2:
                nc.vector.tensor_scalar(share_b[:], alp_all[:, 2:4, :], -0.5, 0.5, ALU.mult, ALU.add)
            for cols in cuts(t):
                nc.vector.tensor_tensor(win_a[t][:, cols], win_a[t][:, S + cols.start : S + cols.stop], share[t][:, cols], ALU.mult)

        def fetch1(t):
            for cols in cuts(t):
                nc.scalar.activation(first[t][:, cols], win_a[t][:].indirect(entries(in1_sb, cols)), ACT.Copy, bias=-0.5)

        def fetch2(t):
            for cols in cuts(t):
                nc.vector.tensor_tensor(over[t][:, cols], win_a[t][:].indirect(entries(in2_sb, cols)), first[t][:, cols], ALU.add)

        def logv(t):
            tag = "share_b" if t == 0 else f"log{t}"
            logs[t] = keep.tile([P, S], F32, name=f"log{t}", tag=tag, align_bytes=64)
            nc.scalar.activation(logs[t][:], over[t][:], ACT.Ln, bias=0.8)

        def massv(t):
            nc.vector.scalar_tensor_tensor(mass[t][:], over[t][:], 0.0, win_a[t][:, S:], ALU.max, ALU.add)

        def estv(t):
            nc.vector.scalar_tensor_tensor(est[:, t, :], mass[t][:], unit_sb[:, t : t + 1], alp_sb[t], ALU.mult, ALU.mult)

        def fetch3(t, lo, hi):
            nc.scalar.activation(logg[:, t, lo:hi], logs[t][:].indirect(in2_sb[:, lo // 16 : hi // 16]), ACT.Copy)

        deal(0, 1)
        product(0)
        deal(1, PACK)
        for t in range(1, PACK):
            product(t)
        absval(0)
        send(0)
        for t in range(PACK):
            if t + 1 < PACK:
                absval(t + 1)
                send(t + 1)
            fetch1(t)
            fetch2(t)
        for t in range(PACK):
            logv(t)
            massv(t)
            estv(t)
        out_v = out.rearrange("(b p) j -> p b j", p=P)
        for h in range(2):
            for t in range(PACK):
                fetch3(t, h * S // 2, (h + 1) * S // 2)
        for c in range(PIECES):
            cols = slice(c * W, (c + 1) * W)
            hid = keep.tile([P, W * PACK], BF16, name=f"hid{c}", align_bytes=64)
            nc.vector.tensor_tensor(
                hid[:].rearrange("p (c i t) -> p c t i", i=4, t=PACK),
                logg[:, :, cols].rearrange("p t (c i) -> p c t i", i=4),
                est[:, :, cols].rearrange("p t (c i) -> p c t i", i=4),
                ALU.mult,
            )
            hw = keep.tile([P, W], U32, name=f"hw{c}", align_bytes=64)
            hs = keep.tile([P, W], U8, name=f"hs{c}", align_bytes=64)
            nc.vector.quantize_mx(out=hw[:].bitcast(FP8X4), scales=hs[:], in_=hid[:])
            res_sb = keep.tile([P, N // P, W], F32, name=f"res_sb{c}", align_bytes=64)
            last = c == PIECES - 1
            if last:
                acc = [psum.tile([P, W], F32, name=f"acc{c}_{b}", tag=f"bank_last{b}")[:] for b in range(N // P)]
            else:
                both = psum.tile([P, N // P, W], F32, name=f"acc{c}", tag=f"bank{c}_0")
                acc = [both[:, b, :] for b in range(N // P)]
            for b in range(N // P):
                nc.tensor.matmul_mx(acc[b], lhsT=w2w[:, 2 * P * b : 2 * P * (b + 1)].bitcast(FP4X4),
                                    lhsT_scale=w2s[:, P * b : P * (b + 1)],
                                    rhs=hw[:].bitcast(FP8X4), rhs_scale=hs[:], start=True, stop=True)
            if last:
                nc.scalar.activation(res_sb[:, 0, :], acc[0], ACT.Copy)
                nc.vector.tensor_copy(res_sb[:, 1, :], acc[1])
            else:
                nc.scalar.activation(res_sb[:], both[:], ACT.Copy)
            nc.sync.dma_start(out=out_v[:, :, cols], in_=res_sb[:])
